import numpy as np
import ml_dtypes

BF16 = ml_dtypes.bfloat16


def bf(x):
    return np.asarray(x, np.float32).astype(BF16)


def f32(x):
    return np.asarray(x, np.float32)


def f64(x):
    return np.asarray(x).astype(np.float64)


def striped(idx):
    return np.tile(idx.reshape(-1, 16).T, (8, 1))


S, K, M, N, E, Q = 512, 128, 256, 256, 4, 64


def setup_inputs():
    return {"base": bf(np.random.standard_normal((M, S))), "x": bf(np.random.standard_normal((K, N))), "w": bf(np.random.standard_normal((E, K, M)) / np.sqrt(K)), "s": f32(0.5 + np.random.random_sample((M, 1))), "b": f32(0.5 * np.random.standard_normal((M, 1))), "offs": striped(np.random.permutation(S)[:N])}


def reference(base, x, w, s, b, offs):
    idx = offs[:16].T.reshape(-1)
    z = f64(base).copy()
    for e in range(E):
        z[:, idx[e * Q : (e + 1) * Q]] = f64(w)[e].T @ f64(x)[:, e * Q : (e + 1) * Q]
    return z * f64(s) + f64(b)

@@ -1,0 +1,61 @@
+import concourse.mybir as mybir
+from concourse.masks import make_identity
+
+BF16, F32, U16 = mybir.dt.bfloat16, mybir.dt.float32, mybir.dt.uint16
+MULT, ADD = mybir.AluOpType.mult, mybir.AluOpType.add
+IDENTITY = mybir.ActivationFunctionType.Identity
+
+P = 128
+TOKENS = 512
+FEATURES = 256
+BLOCKS = FEATURES // P
+EXPERTS = 4
+PIECE = 64
+LIST = EXPERTS * PIECE
+PIECE_COLS = PIECE // 16
+
+FLOPS = 2 * P * FEATURES * LIST
+
+
+def tile_scatter_matmul_kernel(tc, base, x, w, s, b, offs, out):
+    nc = tc.nc
+    with (
+        tc.tile_pool(name="held", bufs=1) as held,
+        tc.psum_pool(name="windows", bufs=1) as windows,
+    ):
+        offsets = held.tile([P, LIST // 16], U16, name="offsets")
+        nc.sync.dma_start(offsets[:], offs)
+        base_sb = held.tile([P, BLOCKS, TOKENS], BF16, name="base_sb")
+        nc.scalar.dma_start(base_sb[:], base.rearrange("(a p) t -> p a t", p=P))
+        x_sb = held.tile([P, LIST], BF16, name="x_sb")
+        nc.sync.dma_start(x_sb[:], x)
+        w_sb = held.tile([P, EXPERTS, FEATURES], BF16, name="w_sb")
+        nc.gpsimd.dma_start(w_sb[:], w.rearrange("e k m -> k e m"))
+        gain = held.tile([P, BLOCKS], F32, name="gain")
+        nc.sync.dma_start(gain[:], s.rearrange("(a p) o -> p (a o)", p=P))
+        shift = held.tile([P, BLOCKS], F32, name="shift")
+        nc.scalar.dma_start(shift[:], b.rearrange("(a p) o -> p (a o)", p=P))
+
+        ident = held.tile([P, P], BF16, name="ident")
+        make_identity(nc, ident[:])
+
+        window = [windows.tile([P, TOKENS], F32, name="window%d" % a) for a in range(BLOCKS)]
+        for a in range(BLOCKS):
+            nc.tensor.matmul(window[a][:], ident[:], base_sb[:, a, :], start=True, stop=True)
+
+        for a in range(BLOCKS):
+            for e in range(EXPERTS):
+                nc.tensor.matmul(
+                    window[a][:].indirect(offsets[:, e * PIECE_COLS : (e + 1) * PIECE_COLS]),
+                    w_sb[:, e, a * P : (a + 1) * P],
+                    x_sb[:, e * PIECE : (e + 1) * PIECE],
+                    start=True,
+                    stop=True,
+                )
+
+        result0 = held.tile([P, TOKENS], F32, name="result0")
+        nc.vector.tensor_scalar(result0[:], window[0][:], gain[:, 0:1], shift[:, 0:1], MULT, ADD)
+        nc.sync.dma_start(out[0:P, :], result0[:])
+        result1 = held.tile([P, TOKENS], F32, name="result1")
+        nc.scalar.activation(result1[:], window[1][:], IDENTITY, bias=shift[:, 1:2], scale=gain[:, 1:2])
+        nc.scalar.dma_start(out[P : 2 * P, :], result1[:])

@@ -23,21 +23,21 @@ def tile_scatter_matmul_kernel(tc, base, x, w, s, b, offs, out):
         tc.tile_pool(name="held", bufs=1) as held,
         tc.psum_pool(name="windows", bufs=1) as windows,
     ):
+        ident = held.tile([P, P], BF16, name="ident")
+        make_identity(nc, ident[:])
+
         offsets = held.tile([P, LIST // 16], U16, name="offsets")
         nc.sync.dma_start(offsets[:], offs)
         base_sb = held.tile([P, BLOCKS, TOKENS], BF16, name="base_sb")
         nc.scalar.dma_start(base_sb[:], base.rearrange("(a p) t -> p a t", p=P))
-        x_sb = held.tile([P, LIST], BF16, name="x_sb")
-        nc.sync.dma_start(x_sb[:], x)
         w_sb = held.tile([P, EXPERTS, FEATURES], BF16, name="w_sb")
-        nc.gpsimd.dma_start(w_sb[:], w.rearrange("e k m -> k e m"))
+        nc.sync.dma_start(w_sb[:], w.rearrange("e k m -> k e m"))
+        x_sb = held.tile([P, LIST], BF16, name="x_sb")
+        nc.scalar.dma_start(x_sb[:], x)
         gain = held.tile([P, BLOCKS], F32, name="gain")
-        nc.sync.dma_start(gain[:], s.rearrange("(a p) o -> p (a o)", p=P))
+        nc.gpsimd.dma_start(gain[:], s.rearrange("(a p) o -> p (a o)", p=P))
         shift = held.tile([P, BLOCKS], F32, name="shift")
-        nc.scalar.dma_start(shift[:], b.rearrange("(a p) o -> p (a o)", p=P))
-
-        ident = held.tile([P, P], BF16, name="ident")
-        make_identity(nc, ident[:])
+        nc.gpsimd.dma_start(shift[:], b.rearrange("(a p) o -> p (a o)", p=P))
 
         window = [windows.tile([P, TOKENS], F32, name="window%d" % a) for a in range(BLOCKS)]
         for a in range(BLOCKS):

@@ -28,20 +28,23 @@ def tile_scatter_matmul_kernel(tc, base, x, w, s, b, offs, out):
 
         offsets = held.tile([P, LIST // 16], U16, name="offsets")
         nc.sync.dma_start(offsets[:], offs)
-        base_sb = held.tile([P, BLOCKS, TOKENS], BF16, name="base_sb")
-        nc.scalar.dma_start(base_sb[:], base.rearrange("(a p) t -> p a t", p=P))
+        base_sb = [held.tile([P, TOKENS], BF16, name="base_sb%d" % a) for a in range(BLOCKS)]
+        nc.scalar.dma_start(base_sb[0][:], base[0:P, :])
+        nc.sync.dma_start(base_sb[1][:], base[P : 2 * P, :])
         w_sb = held.tile([P, EXPERTS, FEATURES], BF16, name="w_sb")
-        nc.sync.dma_start(w_sb[:], w.rearrange("e k m -> k e m"))
+        nc.scalar.dma_start(w_sb[:], w.rearrange("e k m -> k e m"))
         x_sb = held.tile([P, LIST], BF16, name="x_sb")
-        nc.scalar.dma_start(x_sb[:], x)
+        nc.sync.dma_start(x_sb[:], x)
         gain = held.tile([P, BLOCKS], F32, name="gain")
-        nc.gpsimd.dma_start(gain[:], s.rearrange("(a p) o -> p (a o)", p=P))
+        nc.sync.dma_start(gain[:], s.rearrange("(a p) o -> p (a o)", p=P))
         shift = held.tile([P, BLOCKS], F32, name="shift")
-        nc.gpsimd.dma_start(shift[:], b.rearrange("(a p) o -> p (a o)", p=P))
+        nc.scalar.dma_start(shift[:], b.rearrange("(a p) o -> p (a o)", p=P))
 
+        table_primer = held.tile([P, 1], F32, name="table_primer")
+        nc.scalar.activation(table_primer[:], ident[:, 0:1], IDENTITY)
         window = [windows.tile([P, TOKENS], F32, name="window%d" % a) for a in range(BLOCKS)]
         for a in range(BLOCKS):
-            nc.tensor.matmul(window[a][:], ident[:], base_sb[:, a, :], start=True, stop=True)
+            nc.tensor.matmul(window[a][:], ident[:], base_sb[a][:], start=True, stop=True)
 
         for a in range(BLOCKS):
             for e in range(EXPERTS):

@@ -13,6 +13,7 @@ EXPERTS = 4
 PIECE = 64
 LIST = EXPERTS * PIECE
 PIECE_COLS = PIECE // 16
+HALF = TOKENS // 2
 
 FLOPS = 2 * P * FEATURES * LIST
 
@@ -56,9 +57,12 @@ def tile_scatter_matmul_kernel(tc, base, x, w, s, b, offs, out):
                     stop=True,
                 )
 
-        result0 = held.tile([P, TOKENS], F32, name="result0")
-        nc.vector.tensor_scalar(result0[:], window[0][:], gain[:, 0:1], shift[:, 0:1], MULT, ADD)
-        nc.sync.dma_start(out[0:P, :], result0[:])
-        result1 = held.tile([P, TOKENS], F32, name="result1")
-        nc.scalar.activation(result1[:], window[1][:], IDENTITY, bias=shift[:, 1:2], scale=gain[:, 1:2])
-        nc.scalar.dma_start(out[P : 2 * P, :], result1[:])
+        result = [held.tile([P, TOKENS], F32, name="result%d" % a) for a in range(BLOCKS)]
+        for h in range(2):
+            cols = slice(h * HALF, (h + 1) * HALF)
+            nc.vector.tensor_scalar(result[0][:, cols], window[0][:, cols], gain[:, 0:1], shift[:, 0:1], MULT, ADD)
+            nc.sync.dma_start(out[0:P, cols], result[0][:, cols])
+        for h in range(2):
+            cols = slice(h * HALF, (h + 1) * HALF)
+            nc.scalar.activation(result[1][:, cols], window[1][:, cols], IDENTITY, bias=shift[:, 1:2], scale=gain[:, 1:2])
+            nc.scalar.dma_start(out[P : 2 * P, cols], result[1][:, cols])

@@ -14,6 +14,7 @@ PIECE = 64
 LIST = EXPERTS * PIECE
 PIECE_COLS = PIECE // 16
 HALF = TOKENS // 2
+WARM_MATMULS = BLOCKS * TOKENS // P
 
 FLOPS = 2 * P * FEATURES * LIST
 
@@ -43,6 +44,12 @@ def tile_scatter_matmul_kernel(tc, base, x, w, s, b, offs, out):
 
         table_primer = held.tile([P, 1], F32, name="table_primer")
         nc.scalar.activation(table_primer[:], ident[:, 0:1], IDENTITY)
+
+        zeros = held.tile([P, P], BF16, name="zeros")
+        nc.vector.memset(zeros[:], 0.0)
+        warm_bank = windows.tile([P, P], F32, name="warm_bank")
+        for i in range(WARM_MATMULS):
+            nc.tensor.matmul(warm_bank[:], zeros[:], zeros[:], start=True, stop=True)
         window = [windows.tile([P, TOKENS], F32, name="window%d" % a) for a in range(BLOCKS)]
         for a in range(BLOCKS):
             nc.tensor.matmul(window[a][:], ident[:], base_sb[a][:], start=True, stop=True)

@@ -13,7 +13,8 @@ EXPERTS = 4
 PIECE = 64
 LIST = EXPERTS * PIECE
 PIECE_COLS = PIECE // 16
-HALF = TOKENS // 2
+PIECES = 4
+PIECE_TOKENS = TOKENS // PIECES
 WARM_MATMULS = BLOCKS * TOKENS // P
 
 FLOPS = 2 * P * FEATURES * LIST
@@ -65,11 +66,11 @@ def tile_scatter_matmul_kernel(tc, base, x, w, s, b, offs, out):
                 )
 
         result = [held.tile([P, TOKENS], F32, name="result%d" % a) for a in range(BLOCKS)]
-        for h in range(2):
-            cols = slice(h * HALF, (h + 1) * HALF)
+        for h in range(PIECES):
+            cols = slice(h * PIECE_TOKENS, (h + 1) * PIECE_TOKENS)
             nc.vector.tensor_scalar(result[0][:, cols], window[0][:, cols], gain[:, 0:1], shift[:, 0:1], MULT, ADD)
             nc.sync.dma_start(out[0:P, cols], result[0][:, cols])
-        for h in range(2):
-            cols = slice(h * HALF, (h + 1) * HALF)
+        for h in range(PIECES):
+            cols = slice(h * PIECE_TOKENS, (h + 1) * PIECE_TOKENS)
             nc.scalar.activation(result[1][:, cols], window[1][:, cols], IDENTITY, bias=shift[:, 1:2], scale=gain[:, 1:2])
             nc.scalar.dma_start(out[P : 2 * P, cols], result[1][:, cols])

@@ -10,6 +10,7 @@ TOKENS = 512
 FEATURES = 256
 BLOCKS = FEATURES // P
 EXPERTS = 4
+PAIR = 2
 PIECE = 64
 LIST = EXPERTS * PIECE
 PIECE_COLS = PIECE // 16
@@ -35,7 +36,8 @@ def tile_scatter_matmul_kernel(tc, base, x, w, s, b, offs, out):
         nc.scalar.dma_start(base_sb[0][:], base[0:P, :])
         nc.sync.dma_start(base_sb[1][:], base[P : 2 * P, :])
         w_sb = held.tile([P, EXPERTS, FEATURES], BF16, name="w_sb")
-        nc.scalar.dma_start(w_sb[:], w.rearrange("e k m -> k e m"))
+        for first in range(0, EXPERTS, PAIR):
+            nc.scalar.dma_start(w_sb[:, first : first + PAIR, :], w[first : first + PAIR].rearrange("e k m -> k e m"))
         x_sb = held.tile([P, LIST], BF16, name="x_sb")
         nc.sync.dma_start(x_sb[:], x)
         gain = held.tile([P, BLOCKS], F32, name="gain")
@@ -55,15 +57,16 @@ def tile_scatter_matmul_kernel(tc, base, x, w, s, b, offs, out):
         for a in range(BLOCKS):
             nc.tensor.matmul(window[a][:], ident[:], base_sb[a][:], start=True, stop=True)
 
-        for a in range(BLOCKS):
-            for e in range(EXPERTS):
-                nc.tensor.matmul(
-                    window[a][:].indirect(offsets[:, e * PIECE_COLS : (e + 1) * PIECE_COLS]),
-                    w_sb[:, e, a * P : (a + 1) * P],
-                    x_sb[:, e * PIECE : (e + 1) * PIECE],
-                    start=True,
-                    stop=True,
-                )
+        for first in range(0, EXPERTS, PAIR):
+            for a in range(BLOCKS):
+                for e in range(first, first + PAIR):
+                    nc.tensor.matmul(
+                        window[a][:].indirect(offsets[:, e * PIECE_COLS : (e + 1) * PIECE_COLS]),
+                        w_sb[:, e, a * P : (a + 1) * P],
+                        x_sb[:, e * PIECE : (e + 1) * PIECE],
+                        start=True,
+                        stop=True,
+                    )
 
         result = [held.tile([P, TOKENS], F32, name="result%d" % a) for a in range(BLOCKS)]
         for h in range(PIECES):

@@ -16,7 +16,7 @@ LIST = EXPERTS * PIECE
 PIECE_COLS = PIECE // 16
 PIECES = 4
 PIECE_TOKENS = TOKENS // PIECES
-WARM_MATMULS = BLOCKS * TOKENS // P
+WARM_MATMULS = 16
 
 FLOPS = 2 * P * FEATURES * LIST
 

@@ -35,11 +35,11 @@ def tile_scatter_matmul_kernel(tc, base, x, w, s, b, offs, out):
         base_sb = [held.tile([P, TOKENS], BF16, name="base_sb%d" % a) for a in range(BLOCKS)]
         nc.scalar.dma_start(base_sb[0][:], base[0:P, :])
         nc.sync.dma_start(base_sb[1][:], base[P : 2 * P, :])
-        w_sb = held.tile([P, EXPERTS, FEATURES], BF16, name="w_sb")
-        for first in range(0, EXPERTS, PAIR):
-            nc.scalar.dma_start(w_sb[:, first : first + PAIR, :], w[first : first + PAIR].rearrange("e k m -> k e m"))
         x_sb = held.tile([P, LIST], BF16, name="x_sb")
-        nc.sync.dma_start(x_sb[:], x)
+        nc.scalar.dma_start(x_sb[:], x)
+        w_sb = held.tile([P, EXPERTS, FEATURES], BF16, name="w_sb")
+        for queue, first in ((nc.sync, 0), (nc.scalar, PAIR)):
+            queue.dma_start(w_sb[:, first : first + PAIR, :], w[first : first + PAIR].rearrange("e k m -> k e m"))
         gain = held.tile([P, BLOCKS], F32, name="gain")
         nc.sync.dma_start(gain[:], s.rearrange("(a p) o -> p (a o)", p=P))
         shift = held.tile([P, BLOCKS], F32, name="shift")

@@ -57,16 +57,15 @@ def tile_scatter_matmul_kernel(tc, base, x, w, s, b, offs, out):
         for a in range(BLOCKS):
             nc.tensor.matmul(window[a][:], ident[:], base_sb[a][:], start=True, stop=True)
 
-        for first in range(0, EXPERTS, PAIR):
-            for a in range(BLOCKS):
-                for e in range(first, first + PAIR):
-                    nc.tensor.matmul(
-                        window[a][:].indirect(offsets[:, e * PIECE_COLS : (e + 1) * PIECE_COLS]),
-                        w_sb[:, e, a * P : (a + 1) * P],
-                        x_sb[:, e * PIECE : (e + 1) * PIECE],
-                        start=True,
-                        stop=True,
-                    )
+        for a in range(BLOCKS):
+            for e in range(EXPERTS):
+                nc.tensor.matmul(
+                    window[a][:].indirect(offsets[:, e * PIECE_COLS : (e + 1) * PIECE_COLS]),
+                    w_sb[:, e, a * P : (a + 1) * P],
+                    x_sb[:, e * PIECE : (e + 1) * PIECE],
+                    start=True,
+                    stop=True,
+                )
 
         result = [held.tile([P, TOKENS], F32, name="result%d" % a) for a in range(BLOCKS)]
         for h in range(PIECES):

@@ -16,7 +16,7 @@ LIST = EXPERTS * PIECE
 PIECE_COLS = PIECE // 16
 PIECES = 4
 PIECE_TOKENS = TOKENS // PIECES
-WARM_MATMULS = 16
+WARM_MATMULS = BLOCKS * TOKENS // P
 
 FLOPS = 2 * P * FEATURES * LIST
 

@@ -32,18 +32,19 @@ def tile_scatter_matmul_kernel(tc, base, x, w, s, b, offs, out):
 
         offsets = held.tile([P, LIST // 16], U16, name="offsets")
         nc.sync.dma_start(offsets[:], offs)
+        base_rows = base.rearrange("(p a) t -> p a t", a=BLOCKS)
         base_sb = [held.tile([P, TOKENS], BF16, name="base_sb%d" % a) for a in range(BLOCKS)]
-        nc.scalar.dma_start(base_sb[0][:], base[0:P, :])
-        nc.sync.dma_start(base_sb[1][:], base[P : 2 * P, :])
+        nc.scalar.dma_start(base_sb[0][:], base_rows[:, 0, :])
+        nc.sync.dma_start(base_sb[1][:], base_rows[:, 1, :])
         x_sb = held.tile([P, LIST], BF16, name="x_sb")
         nc.scalar.dma_start(x_sb[:], x)
         w_sb = held.tile([P, EXPERTS, FEATURES], BF16, name="w_sb")
         for queue, first in ((nc.sync, 0), (nc.scalar, PAIR)):
             queue.dma_start(w_sb[:, first : first + PAIR, :], w[first : first + PAIR].rearrange("e k m -> k e m"))
         gain = held.tile([P, BLOCKS], F32, name="gain")
-        nc.sync.dma_start(gain[:], s.rearrange("(a p) o -> p (a o)", p=P))
+        nc.sync.dma_start(gain[:], s.rearrange("(p a) o -> p (a o)", a=BLOCKS))
         shift = held.tile([P, BLOCKS], F32, name="shift")
-        nc.scalar.dma_start(shift[:], b.rearrange("(a p) o -> p (a o)", p=P))
+        nc.scalar.dma_start(shift[:], b.rearrange("(p a) o -> p (a o)", a=BLOCKS))
 
         table_primer = held.tile([P, 1], F32, name="table_primer")
         nc.scalar.activation(table_primer[:], ident[:, 0:1], IDENTITY)
@@ -61,18 +62,19 @@ def tile_scatter_matmul_kernel(tc, base, x, w, s, b, offs, out):
             for e in range(EXPERTS):
                 nc.tensor.matmul(
                     window[a][:].indirect(offsets[:, e * PIECE_COLS : (e + 1) * PIECE_COLS]),
-                    w_sb[:, e, a * P : (a + 1) * P],
+                    w_sb[:, e, a:FEATURES:BLOCKS],
                     x_sb[:, e * PIECE : (e + 1) * PIECE],
                     start=True,
                     stop=True,
                 )
 
+        out_rows = out.rearrange("(p a) t -> p a t", a=BLOCKS)
         result = [held.tile([P, TOKENS], F32, name="result%d" % a) for a in range(BLOCKS)]
         for h in range(PIECES):
             cols = slice(h * PIECE_TOKENS, (h + 1) * PIECE_TOKENS)
             nc.vector.tensor_scalar(result[0][:, cols], window[0][:, cols], gain[:, 0:1], shift[:, 0:1], MULT, ADD)
-            nc.sync.dma_start(out[0:P, cols], result[0][:, cols])
+            nc.sync.dma_start(out_rows[:, 0, cols], result[0][:, cols])
         for h in range(PIECES):
             cols = slice(h * PIECE_TOKENS, (h + 1) * PIECE_TOKENS)
             nc.scalar.activation(result[1][:, cols], window[1][:, cols], IDENTITY, bias=shift[:, 1:2], scale=gain[:, 1:2])
-            nc.scalar.dma_start(out[P : 2 * P, cols], result[1][:, cols])
+            nc.scalar.dma_start(out_rows[:, 1, cols], result[1][:, cols])

import concourse.mybir as mybir
from concourse.masks import make_identity

BF16, F32, U16 = mybir.dt.bfloat16, mybir.dt.float32, mybir.dt.uint16
MULT, ADD = mybir.AluOpType.mult, mybir.AluOpType.add
IDENTITY = mybir.ActivationFunctionType.Identity

P = 128
TOKENS = 512
FEATURES = 256
BLOCKS = FEATURES // P
EXPERTS = 4
PAIR = 2
PIECE = 64
LIST = EXPERTS * PIECE
PIECE_COLS = PIECE // 16
PIECES = 4
PIECE_TOKENS = TOKENS // PIECES
WARM_MATMULS = BLOCKS * TOKENS // P

FLOPS = 2 * P * FEATURES * LIST


def tile_scatter_matmul_kernel(tc, base, x, w, s, b, offs, out):
    nc = tc.nc
    with (
        tc.tile_pool(name="held", bufs=1) as held,
        tc.psum_pool(name="windows", bufs=1) as windows,
    ):
        ident = held.tile([P, P], BF16, name="ident")
        make_identity(nc, ident[:])

        offsets = held.tile([P, LIST // 16], U16, name="offsets")
        nc.sync.dma_start(offsets[:], offs)
        base_rows = base.rearrange("(p a) t -> p a t", a=BLOCKS)
        base_sb = [held.tile([P, TOKENS], BF16, name="base_sb%d" % a) for a in range(BLOCKS)]
        nc.scalar.dma_start(base_sb[0][:], base_rows[:, 0, :])
        nc.sync.dma_start(base_sb[1][:], base_rows[:, 1, :])
        x_sb = held.tile([P, LIST], BF16, name="x_sb")
        nc.scalar.dma_start(x_sb[:], x)
        w_sb = held.tile([P, EXPERTS, FEATURES], BF16, name="w_sb")
        for queue, first in ((nc.sync, 0), (nc.scalar, PAIR)):
            queue.dma_start(w_sb[:, first : first + PAIR, :], w[first : first + PAIR].rearrange("e k m -> k e m"))
        gain = held.tile([P, BLOCKS], F32, name="gain")
        nc.sync.dma_start(gain[:], s.rearrange("(p a) o -> p (a o)", a=BLOCKS))
        shift = held.tile([P, BLOCKS], F32, name="shift")
        nc.scalar.dma_start(shift[:], b.rearrange("(p a) o -> p (a o)", a=BLOCKS))

        table_primer = held.tile([P, 1], F32, name="table_primer")
        nc.scalar.activation(table_primer[:], ident[:, 0:1], IDENTITY)

        zeros = held.tile([P, P], BF16, name="zeros")
        nc.vector.memset(zeros[:], 0.0)
        warm_bank = windows.tile([P, P], F32, name="warm_bank")
        for i in range(WARM_MATMULS):
            nc.tensor.matmul(warm_bank[:], zeros[:], zeros[:], start=True, stop=True)
        window = [windows.tile([P, TOKENS], F32, name="window%d" % a) for a in range(BLOCKS)]
        for a in range(BLOCKS):
            nc.tensor.matmul(window[a][:], ident[:], base_sb[a][:], start=True, stop=True)

        for a in range(BLOCKS):
            for e in range(EXPERTS):
                nc.tensor.matmul(
                    window[a][:].indirect(offsets[:, e * PIECE_COLS : (e + 1) * PIECE_COLS]),
                    w_sb[:, e, a:FEATURES:BLOCKS],
                    x_sb[:, e * PIECE : (e + 1) * PIECE],
                    start=True,
                    stop=True,
                )

        out_rows = out.rearrange("(p a) t -> p a t", a=BLOCKS)
        result = [held.tile([P, TOKENS], F32, name="result%d" % a) for a in range(BLOCKS)]
        for h in range(PIECES):
            cols = slice(h * PIECE_TOKENS, (h + 1) * PIECE_TOKENS)
            nc.vector.tensor_scalar(result[0][:, cols], window[0][:, cols], gain[:, 0:1], shift[:, 0:1], MULT, ADD)
            nc.sync.dma_start(out_rows[:, 0, cols], result[0][:, cols])
        for h in range(PIECES):
            cols = slice(h * PIECE_TOKENS, (h + 1) * PIECE_TOKENS)
            nc.scalar.activation(result[1][:, cols], window[1][:, cols], IDENTITY, bias=shift[:, 1:2], scale=gain[:, 1:2])
            nc.scalar.dma_start(out_rows[:, 1, cols], result[1][:, cols])
